import numpy as np
import ml_dtypes


def mxq(x, axis, fmt="e4m3"):
    dtype, down = {"e4m3": (ml_dtypes.float8_e4m3fn, 7), "e5m2": (ml_dtypes.float8_e5m2, 14)}[fmt]
    v = np.moveaxis(np.asarray(x, np.float32).astype(ml_dtypes.bfloat16).astype(np.float64), axis, -1)
    blocks = v.reshape(v.shape[:-1] + (-1, 32))
    amax = np.abs(blocks).max(-1, keepdims=True)
    byte = np.maximum(np.where(amax > 0, np.frexp(amax)[1] - 1 + 127, 0) - down, 1)
    scale = np.exp2(byte - 127.0)
    codes = (blocks / scale).astype(np.float32).astype(dtype).astype(np.float64)
    return np.moveaxis((codes * scale).reshape(v.shape), -1, axis)


WIDE = False


def mx_kscale(k):
    if not WIDE:
        return np.ones(k)
    levels = np.array([10, -10, 5, -5, 0])
    if k % 512:
        return np.exp2(np.random.permutation(np.resize(levels, k // 32))).repeat(32)
    a = np.empty((k // 512, 16))
    for p in range(k // 512):
        a[p, :8] = np.random.permutation(np.resize(levels, 8))
        for g in range(8):
            far = levels[np.abs(levels - a[p, g]) >= 10]
            a[p, g + 8] = far[np.random.randint(len(far))]
    return np.exp2(a.ravel()).repeat(32)


def f64(x):
    return np.asarray(x).astype(np.float64)


def striped8(idx):
    return np.concatenate([v.reshape(-1, 16).T for v in idx]).astype(np.uint16)


def unstriped8(offs):
    return np.stack([offs[16 * g:16 * g + 16].T.reshape(-1) for g in range(8)]).astype(np.int64)


K, M, T, S = 1024, 256, 1024, 512


def setup_inputs():
    n = np.random.standard_normal
    s = mx_kscale(K)[:, None]
    return {
        "xT": (n((K, T)) * s).astype(np.float32),
        "w": (n((K, M)) / np.sqrt(K) / s).astype(np.float32),
        "wgt": np.repeat(np.random.uniform(0.5, 2.0, (8, S)), 16, axis=0).astype(np.float32),
        "wgo": np.repeat(np.random.uniform(0.5, 2.0, (8, S)), 16, axis=0).astype(np.float32),
        "offs": striped8(np.stack([np.random.permutation(T)[:S] for _ in range(8)])),
        "offs2": striped8(np.stack([np.random.permutation(T)[:S] for _ in range(8)])),
    }


def reference(xT, w, wgt, wgo, offs, offs2):
    idx = unstriped8(offs)
    group = np.arange(K) % 512 // 64
    xg = f64(wgt)[np.arange(K) // 4 % 128] * f64(xT)[np.arange(K)[:, None], idx[group]]
    xT_ = mxq(xg, 0, "e4m3")
    w_ = mxq(f64(w), 0, "e4m3")
    y = w_.T @ xT_
    place = unstriped8(offs2)[np.arange(M) % 128 // 16]
    out = np.zeros((M, T))
    out[np.arange(M)[:, None], place] = f64(wgo)[np.arange(M) % 128] * (y)
    return out

@@ -1,0 +1,156 @@
+from contextlib import ExitStack
+
+import concourse.mybir as mybir
+
+K, M, T, S = 1024, 256, 1024, 512
+FLOPS = 2 * K * M * S
+
+F32 = mybir.dt.float32
+BF16 = mybir.dt.bfloat16
+U32 = mybir.dt.uint32
+U16 = mybir.dt.uint16
+U8 = mybir.dt.uint8
+FP8X4 = mybir.dt.float8_e4m3fn_x4
+MULT = mybir.AluOpType.mult
+
+P = 128
+PACK = 4
+PASSES = K // (P * PACK)
+HALVES = 2
+N = S // HALVES
+M_TILES = M // P
+LIST_COLS = N // 16
+
+
+def tile_list_hboth_none_kernel(tc, xT, w, wgt, wgo, offs, offs2, out):
+    nc = tc.nc
+    x_planes = xT.rearrange("(a p i) t -> a i p t", a=PASSES, i=PACK)
+    w_passes = w.rearrange("(a p i) n -> a p i n", a=PASSES, i=PACK)
+
+    with ExitStack() as ctx:
+        keep = ctx.enter_context(tc.tile_pool(name="keep", bufs=1))
+        psum = ctx.enter_context(tc.psum_pool(name="psum", bufs=1))
+
+        def cols(h):
+            return slice(h * N, (h + 1) * N)
+
+        offsets = keep.tile([P, S // 16], U16, name="offsets")
+        offsets2 = keep.tile([P, S // 16], U16, name="offsets2")
+        planes = [[keep.tile([P, T], F32, name=f"x{a}{i}") for i in range(PACK)] for a in range(PASSES)]
+        weights = [keep.tile([P, N], F32, name=f"wgt{h}") for h in range(HALVES)]
+        w_raw = [keep.tile([P, PACK, M], F32, name=f"wraw{a}") for a in range(PASSES)]
+        out_weights = keep.tile([P, S], F32, name="wgo_sb")
+        placed = [keep.tile([P, T], F32, name=f"placed{m}") for m in range(M_TILES)]
+
+        def load_plane(a, i):
+            nc.sync.dma_start(out=planes[a][i][:], in_=x_planes[a, i])
+
+        def load_w(a):
+            nc.sync.dma_start(out=w_raw[a][:], in_=w_passes[a])
+
+        nc.sync.dma_start(offsets[:], offs)
+        nc.sync.dma_start(out=weights[0][:], in_=wgt[:, cols(0)])
+        load_plane(0, 0)
+        nc.sync.dma_start(out=weights[1][:], in_=wgt[:, cols(1)])
+        load_plane(0, 1)
+        load_plane(0, 2)
+        load_plane(0, 3)
+        load_w(0)
+        load_plane(1, 0)
+        load_plane(1, 1)
+        load_w(1)
+        load_plane(1, 2)
+        load_plane(1, 3)
+        nc.sync.dma_start(offsets2[:], offs2)
+        nc.sync.dma_start(out=out_weights[:], in_=wgo)
+
+        for m in range(M_TILES):
+            nc.vector.memset(placed[m][:], 0.0)
+
+        gathered = [[keep.tile([P, PACK, N], F32, name=f"g{a}{h}") for h in range(HALVES)] for a in range(PASSES)]
+        grouped = [[keep.tile([P, N, PACK], BF16, name=f"gr{a}{h}", align_bytes=64) for h in range(HALVES)] for a in range(PASSES)]
+        x_codes = [[keep.tile([P, N], U32, name=f"xc{a}{h}", align_bytes=64) for h in range(HALVES)] for a in range(PASSES)]
+        x_scales = [[keep.tile([P, N], U8, name=f"xs{a}{h}", align_bytes=64) for h in range(HALVES)] for a in range(PASSES)]
+        w_grouped = [keep.tile([P, M, PACK], BF16, name=f"wg{a}", align_bytes=64) for a in range(PASSES)]
+        w_codes = [keep.tile([P, M], U32, name=f"wc{a}", align_bytes=64) for a in range(PASSES)]
+        w_scales = [keep.tile([P, M], U8, name=f"ws{a}", align_bytes=64) for a in range(PASSES)]
+
+        def gather(a, i, h):
+            nc.vector.tensor_tensor(
+                gathered[a][h][:, i, :],
+                planes[a][i][:].indirect(offsets[:, h * LIST_COLS : (h + 1) * LIST_COLS]),
+                weights[h][:],
+                MULT,
+            )
+
+        def interleave(dst, src):
+            nc.scalar.copy(
+                out=dst[:].rearrange("p (c j) i -> p c i j", j=4),
+                in_=src[:].rearrange("p i (c j) -> p c i j", j=4),
+            )
+
+        def quantize(codes, scales, src):
+            nc.vector.quantize_mx(
+                out=codes[:].bitcast(FP8X4),
+                scales=scales[:],
+                in_=src[:].rearrange("p n i -> p (n i)"),
+            )
+
+        def product(m, h):
+            acc = psum.tile([P, N], F32, name=f"acc{m}{h}")
+            m_cols = slice(m * P, (m + 1) * P)
+            for a in range(PASSES):
+                nc.tensor.matmul_mx(
+                    out=acc[:],
+                    lhsT=w_codes[a][:, m_cols].bitcast(FP8X4),
+                    lhsT_scale=w_scales[a][:, m_cols],
+                    rhs=x_codes[a][h][:].bitcast(FP8X4),
+                    rhs_scale=x_scales[a][h][:],
+                    start=(a == 0),
+                    stop=(a == PASSES - 1),
+                )
+            y = keep.tile([P, N], F32, name=f"y{m}{h}")
+            nc.scalar.copy(out=y[:], in_=acc[:])
+            return y
+
+        def scatter(m, h, y):
+            nc.vector.tensor_tensor(
+                placed[m][:].indirect(offsets2[:, h * LIST_COLS : (h + 1) * LIST_COLS]),
+                y[:],
+                out_weights[:, cols(h)],
+                MULT,
+            )
+
+        for i in range(PACK):
+            gather(0, i, 0)
+            gather(0, i, 1)
+        interleave(grouped[0][0], gathered[0][0])
+        interleave(grouped[0][1], gathered[0][1])
+        interleave(w_grouped[0], w_raw[0])
+        gather(1, 0, 0)
+        gather(1, 0, 1)
+        quantize(x_codes[0][0], x_scales[0][0], grouped[0][0])
+        gather(1, 1, 0)
+        gather(1, 1, 1)
+        quantize(x_codes[0][1], x_scales[0][1], grouped[0][1])
+        quantize(w_codes[0], w_scales[0], w_grouped[0])
+        interleave(w_grouped[1], w_raw[1])
+        gather(1, 2, 0)
+        gather(1, 3, 0)
+        interleave(grouped[1][0], gathered[1][0])
+        quantize(w_codes[1], w_scales[1], w_grouped[1])
+        gather(1, 2, 1)
+        gather(1, 3, 1)
+        quantize(x_codes[1][0], x_scales[1][0], grouped[1][0])
+        y00 = product(0, 0)
+        y10 = product(1, 0)
+        interleave(grouped[1][1], gathered[1][1])
+        scatter(0, 0, y00)
+        quantize(x_codes[1][1], x_scales[1][1], grouped[1][1])
+        scatter(1, 0, y10)
+        y01 = product(0, 1)
+        y11 = product(1, 1)
+        scatter(0, 1, y01)
+        nc.sync.dma_start(out=out[0:P, :], in_=placed[0][:])
+        scatter(1, 1, y11)
+        nc.sync.dma_start(out=out[P : 2 * P, :], in_=placed[1][:])

@@ -38,9 +38,18 @@ def tile_list_hboth_none_kernel(tc, xT, w, wgt, wgo, offs, offs2, out):
         offsets2 = keep.tile([P, S // 16], U16, name="offsets2")
         planes = [[keep.tile([P, T], F32, name=f"x{a}{i}") for i in range(PACK)] for a in range(PASSES)]
         weights = [keep.tile([P, N], F32, name=f"wgt{h}") for h in range(HALVES)]
+        late_weights = keep.tile([P, N], F32, name="wgt1_late")
         w_raw = [keep.tile([P, PACK, M], F32, name=f"wraw{a}") for a in range(PASSES)]
         out_weights = keep.tile([P, S], F32, name="wgo_sb")
         placed = [keep.tile([P, T], F32, name=f"placed{m}") for m in range(M_TILES)]
+
+        x_codes = [[keep.tile([P, N], U32, name=f"xc{a}{h}", align_bytes=64) for h in range(HALVES)] for a in range(PASSES)]
+        x_scales = [[keep.tile([P, N], U8, name=f"xs{a}{h}", align_bytes=64) for h in range(HALVES)] for a in range(PASSES)]
+        w_grouped = [keep.tile([P, M, PACK], BF16, name=f"wg{a}", align_bytes=64) for a in range(PASSES)]
+        w_codes = [keep.tile([P, M], U32, name=f"wc{a}", align_bytes=64) for a in range(PASSES)]
+        w_scales = [keep.tile([P, M], U8, name=f"ws{a}", align_bytes=64) for a in range(PASSES)]
+        accs = [[psum.tile([P, N], F32, name=f"acc{m}{h}") for h in range(HALVES)] for m in range(M_TILES)]
+        ys = [[keep.tile([P, N], F32, name=f"y{m}{h}") for h in range(HALVES)] for m in range(M_TILES)]
 
         def load_plane(a, i):
             nc.sync.dma_start(out=planes[a][i][:], in_=x_planes[a, i])
@@ -48,109 +57,144 @@ def tile_list_hboth_none_kernel(tc, xT, w, wgt, wgo, offs, offs2, out):
         def load_w(a):
             nc.sync.dma_start(out=w_raw[a][:], in_=w_passes[a])
 
-        nc.sync.dma_start(offsets[:], offs)
-        nc.sync.dma_start(out=weights[0][:], in_=wgt[:, cols(0)])
-        load_plane(0, 0)
-        nc.sync.dma_start(out=weights[1][:], in_=wgt[:, cols(1)])
-        load_plane(0, 1)
-        load_plane(0, 2)
-        load_plane(0, 3)
-        load_w(0)
-        load_plane(1, 0)
-        load_plane(1, 1)
-        load_w(1)
-        load_plane(1, 2)
-        load_plane(1, 3)
-        nc.sync.dma_start(offsets2[:], offs2)
-        nc.sync.dma_start(out=out_weights[:], in_=wgo)
+        def load_wgt(h):
+            nc.sync.dma_start(out=weights[h][:], in_=wgt[:, cols(h)])
 
-        for m in range(M_TILES):
-            nc.vector.memset(placed[m][:], 0.0)
+        def load_late():
+            nc.sync.dma_start(out=late_weights[:], in_=wgt[:, cols(1)])
 
         gathered = [[keep.tile([P, PACK, N], F32, name=f"g{a}{h}") for h in range(HALVES)] for a in range(PASSES)]
         grouped = [[keep.tile([P, N, PACK], BF16, name=f"gr{a}{h}", align_bytes=64) for h in range(HALVES)] for a in range(PASSES)]
-        x_codes = [[keep.tile([P, N], U32, name=f"xc{a}{h}", align_bytes=64) for h in range(HALVES)] for a in range(PASSES)]
-        x_scales = [[keep.tile([P, N], U8, name=f"xs{a}{h}", align_bytes=64) for h in range(HALVES)] for a in range(PASSES)]
-        w_grouped = [keep.tile([P, M, PACK], BF16, name=f"wg{a}", align_bytes=64) for a in range(PASSES)]
-        w_codes = [keep.tile([P, M], U32, name=f"wc{a}", align_bytes=64) for a in range(PASSES)]
-        w_scales = [keep.tile([P, M], U8, name=f"ws{a}", align_bytes=64) for a in range(PASSES)]
+        halves = [keep.tile([P, N // 2, PACK], BF16, name=f"half{q}", align_bytes=64) for q in range(2)]
 
-        def gather(a, i, h):
+        def gather(a, i, h, late=None):
             nc.vector.tensor_tensor(
                 gathered[a][h][:, i, :],
                 planes[a][i][:].indirect(offsets[:, h * LIST_COLS : (h + 1) * LIST_COLS]),
-                weights[h][:],
+                (weights[h] if late is None else late_weights)[:],
                 MULT,
             )
 
-        def interleave(dst, src):
+        def int_x(a, h, copy=nc.scalar.copy):
+            copy(
+                out=grouped[a][h][:].rearrange("p (c j) i -> p c i j", j=4),
+                in_=gathered[a][h][:].rearrange("p i (c j) -> p c i j", j=4),
+            )
+
+        def int_half(q, copy):
+            copy(
+                out=halves[q][:].rearrange("p (c j) i -> p c i j", j=4),
+                in_=gathered[1][0][:, :, q * 128 : (q + 1) * 128].rearrange("p i (c j) -> p c i j", j=4),
+            )
+
+        def q_half(q):
+            c = slice(q * 128, (q + 1) * 128)
+            quantize(x_codes[1][0][:, c], x_scales[1][0][:, c], halves[q])
+
+        def int_w(a):
             nc.scalar.copy(
-                out=dst[:].rearrange("p (c j) i -> p c i j", j=4),
-                in_=src[:].rearrange("p i (c j) -> p c i j", j=4),
+                out=w_grouped[a][:].rearrange("p (c j) i -> p c i j", j=4),
+                in_=w_raw[a][:].rearrange("p i (c j) -> p c i j", j=4),
             )
 
         def quantize(codes, scales, src):
-            nc.vector.quantize_mx(
-                out=codes[:].bitcast(FP8X4),
-                scales=scales[:],
-                in_=src[:].rearrange("p n i -> p (n i)"),
+            nc.vector.quantize_mx(out=codes[:].bitcast(FP8X4), scales=scales[:], in_=src[:].rearrange("p n i -> p (n i)"))
+
+        def q_x(a, h):
+            quantize(x_codes[a][h], x_scales[a][h], grouped[a][h])
+
+        def q_w(a):
+            quantize(w_codes[a], w_scales[a], w_grouped[a])
+
+        def mm(a, m, h):
+            m_cols = slice(m * P, (m + 1) * P)
+            nc.tensor.matmul_mx(
+                out=accs[m][h][:],
+                lhsT=w_codes[a][:, m_cols].bitcast(FP8X4),
+                lhsT_scale=w_scales[a][:, m_cols],
+                rhs=x_codes[a][h][:].bitcast(FP8X4),
+                rhs_scale=x_scales[a][h][:],
+                start=(a == 0),
+                stop=(a == PASSES - 1),
             )
 
-        def product(m, h):
-            acc = psum.tile([P, N], F32, name=f"acc{m}{h}")
-            m_cols = slice(m * P, (m + 1) * P)
-            for a in range(PASSES):
-                nc.tensor.matmul_mx(
-                    out=acc[:],
-                    lhsT=w_codes[a][:, m_cols].bitcast(FP8X4),
-                    lhsT_scale=w_scales[a][:, m_cols],
-                    rhs=x_codes[a][h][:].bitcast(FP8X4),
-                    rhs_scale=x_scales[a][h][:],
-                    start=(a == 0),
-                    stop=(a == PASSES - 1),
-                )
-            y = keep.tile([P, N], F32, name=f"y{m}{h}")
-            nc.scalar.copy(out=y[:], in_=acc[:])
-            return y
+        def take(m, h, copy=nc.scalar.copy):
+            copy(out=ys[m][h][:], in_=accs[m][h][:])
 
-        def scatter(m, h, y):
+        def scatter(m, h):
             nc.vector.tensor_tensor(
                 placed[m][:].indirect(offsets2[:, h * LIST_COLS : (h + 1) * LIST_COLS]),
-                y[:],
+                ys[m][h][:],
                 out_weights[:, cols(h)],
                 MULT,
             )
 
-        for i in range(PACK):
-            gather(0, i, 0)
-            gather(0, i, 1)
-        interleave(grouped[0][0], gathered[0][0])
-        interleave(grouped[0][1], gathered[0][1])
-        interleave(w_grouped[0], w_raw[0])
+        def store(m):
+            nc.sync.dma_start(out=out[m * P : (m + 1) * P, :], in_=placed[m][:])
+
+        nc.sync.dma_start(offsets[:], offs)
+        load_wgt(0)
+        load_plane(0, 0)
+        load_wgt(1)
+        load_plane(0, 1)
+        load_plane(0, 2)
+        load_plane(0, 3)
+        load_plane(1, 0)
+        load_plane(1, 1)
+        load_w(0)
+        load_plane(1, 2)
+        load_w(1)
+        load_plane(1, 3)
+        load_late()
+        nc.sync.dma_start(offsets2[:], offs2)
+        nc.sync.dma_start(out=out_weights[:], in_=wgo)
+        nc.vector.memset(placed[0][:], 0.0)
+        nc.vector.memset(placed[1][:], 0.0)
+        gather(0, 0, 0)
+        gather(0, 0, 1)
+        gather(0, 1, 0)
+        gather(0, 1, 1)
+        gather(0, 2, 0)
+        gather(0, 2, 1)
+        gather(0, 3, 0)
+        int_x(0, 0)
+        gather(0, 3, 1)
+        int_x(0, 1)
         gather(1, 0, 0)
         gather(1, 0, 1)
-        quantize(x_codes[0][0], x_scales[0][0], grouped[0][0])
+        q_x(0, 0)
+        int_w(0)
         gather(1, 1, 0)
         gather(1, 1, 1)
-        quantize(x_codes[0][1], x_scales[0][1], grouped[0][1])
-        quantize(w_codes[0], w_scales[0], w_grouped[0])
-        interleave(w_grouped[1], w_raw[1])
+        q_x(0, 1)
         gather(1, 2, 0)
-        gather(1, 3, 0)
-        interleave(grouped[1][0], gathered[1][0])
-        quantize(w_codes[1], w_scales[1], w_grouped[1])
         gather(1, 2, 1)
-        gather(1, 3, 1)
-        quantize(x_codes[1][0], x_scales[1][0], grouped[1][0])
-        y00 = product(0, 0)
-        y10 = product(1, 0)
-        interleave(grouped[1][1], gathered[1][1])
-        scatter(0, 0, y00)
-        quantize(x_codes[1][1], x_scales[1][1], grouped[1][1])
-        scatter(1, 0, y10)
-        y01 = product(0, 1)
-        y11 = product(1, 1)
-        scatter(0, 1, y01)
-        nc.sync.dma_start(out=out[0:P, :], in_=placed[0][:])
-        scatter(1, 1, y11)
-        nc.sync.dma_start(out=out[P : 2 * P, :], in_=placed[1][:])
+        q_w(0)
+        int_w(1)
+        mm(0, 0, 0)
+        mm(0, 1, 0)
+        gather(1, 3, 0)
+        int_half(0, nc.scalar.copy)
+        int_half(1, nc.vector.tensor_copy)
+        q_w(1)
+        q_half(1)
+        q_half(0)
+        mm(1, 0, 0)
+        take(0, 0)
+        mm(1, 1, 0)
+        take(1, 0)
+        gather(1, 3, 1, "late")
+        int_x(1, 1, nc.vector.tensor_copy)
+        mm(0, 0, 1)
+        mm(0, 1, 1)
+        scatter(0, 0)
+        q_x(1, 1)
+        mm(1, 0, 1)
+        take(0, 1)
+        mm(1, 1, 1)
+        take(1, 1)
+        scatter(1, 0)
+        scatter(0, 1)
+        store(0)
+        scatter(1, 1)
+        store(1)

@@ -45,9 +45,10 @@ def tile_list_hboth_none_kernel(tc, xT, w, wgt, wgo, offs, offs2, out):
 
         x_codes = [[keep.tile([P, N], U32, name=f"xc{a}{h}", align_bytes=64) for h in range(HALVES)] for a in range(PASSES)]
         x_scales = [[keep.tile([P, N], U8, name=f"xs{a}{h}", align_bytes=64) for h in range(HALVES)] for a in range(PASSES)]
-        w_grouped = [keep.tile([P, M, PACK], BF16, name=f"wg{a}", align_bytes=64) for a in range(PASSES)]
+        w_grouped = [[keep.tile([P, P, PACK], BF16, name=f"wg{a}{m}", align_bytes=64) for m in range(M_TILES)] for a in range(PASSES)]
         w_codes = [keep.tile([P, M], U32, name=f"wc{a}", align_bytes=64) for a in range(PASSES)]
         w_scales = [keep.tile([P, M], U8, name=f"ws{a}", align_bytes=64) for a in range(PASSES)]
+        w_whole = keep.tile([P, M, PACK], BF16, name="w_whole", align_bytes=64)
         accs = [[psum.tile([P, N], F32, name=f"acc{m}{h}") for h in range(HALVES)] for m in range(M_TILES)]
         ys = [[keep.tile([P, N], F32, name=f"y{m}{h}") for h in range(HALVES)] for m in range(M_TILES)]
 
@@ -91,10 +92,11 @@ def tile_list_hboth_none_kernel(tc, xT, w, wgt, wgo, offs, offs2, out):
             c = slice(q * 128, (q + 1) * 128)
             quantize(x_codes[1][0][:, c], x_scales[1][0][:, c], halves[q])
 
-        def int_w(a):
-            nc.scalar.copy(
-                out=w_grouped[a][:].rearrange("p (c j) i -> p c i j", j=4),
-                in_=w_raw[a][:].rearrange("p i (c j) -> p c i j", j=4),
+        def int_w(a, m=None, copy=nc.scalar.copy):
+            src = w_raw[a][:] if m is None else w_raw[a][:, :, m * P : (m + 1) * P]
+            copy(
+                out=(w_whole if m is None else w_grouped[a][m])[:].rearrange("p (c j) i -> p c i j", j=4),
+                in_=src.rearrange("p i (c j) -> p c i j", j=4),
             )
 
         def quantize(codes, scales, src):
@@ -103,8 +105,9 @@ def tile_list_hboth_none_kernel(tc, xT, w, wgt, wgo, offs, offs2, out):
         def q_x(a, h):
             quantize(x_codes[a][h], x_scales[a][h], grouped[a][h])
 
-        def q_w(a):
-            quantize(w_codes[a], w_scales[a], w_grouped[a])
+        def q_w(a, m=None):
+            c = slice(0, M) if m is None else slice(m * P, (m + 1) * P)
+            quantize(w_codes[a][:, c], w_scales[a][:, c], w_whole if m is None else w_grouped[a][m])
 
         def mm(a, m, h):
             m_cols = slice(m * P, (m + 1) * P)
@@ -141,10 +144,10 @@ def tile_list_hboth_none_kernel(tc, xT, w, wgt, wgo, offs, offs2, out):
         load_plane(0, 3)
         load_plane(1, 0)
         load_plane(1, 1)
-        load_w(0)
         load_plane(1, 2)
-        load_w(1)
+        load_w(0)
         load_plane(1, 3)
+        load_w(1)
         load_late()
         nc.sync.dma_start(offsets2[:], offs2)
         nc.sync.dma_start(out=out_weights[:], in_=wgo)
@@ -170,21 +173,23 @@ def tile_list_hboth_none_kernel(tc, xT, w, wgt, wgo, offs, offs2, out):
         gather(1, 2, 0)
         gather(1, 2, 1)
         q_w(0)
-        int_w(1)
         mm(0, 0, 0)
         mm(0, 1, 0)
         gather(1, 3, 0)
         int_half(0, nc.scalar.copy)
         int_half(1, nc.vector.tensor_copy)
-        q_w(1)
+        int_w(1, 0, nc.vector.tensor_copy)
+        int_w(1, 1)
+        q_w(1, 0)
+        q_w(1, 1)
         q_half(1)
         q_half(0)
         mm(1, 0, 0)
-        take(0, 0)
+        take(0, 0, nc.vector.tensor_copy)
         mm(1, 1, 0)
         take(1, 0)
         gather(1, 3, 1, "late")
-        int_x(1, 1, nc.vector.tensor_copy)
+        int_x(1, 1)
         mm(0, 0, 1)
         mm(0, 1, 1)
         scatter(0, 0)

@@ -43,8 +43,8 @@ def tile_list_hboth_none_kernel(tc, xT, w, wgt, wgo, offs, offs2, out):
         out_weights = keep.tile([P, S], F32, name="wgo_sb")
         placed = [keep.tile([P, T], F32, name=f"placed{m}") for m in range(M_TILES)]
 
-        x_codes = [[keep.tile([P, N], U32, name=f"xc{a}{h}", align_bytes=64) for h in range(HALVES)] for a in range(PASSES)]
-        x_scales = [[keep.tile([P, N], U8, name=f"xs{a}{h}", align_bytes=64) for h in range(HALVES)] for a in range(PASSES)]
+        x_codes = [[keep.tile([P, N], U32, name=f"xc{a}{h}", align_bytes=64) if a else None for h in range(HALVES)] for a in range(PASSES)]
+        x_scales = [[keep.tile([P, N], U8, name=f"xs{a}{h}", align_bytes=64) if a else None for h in range(HALVES)] for a in range(PASSES)]
         w_grouped = [[keep.tile([P, P, PACK], BF16, name=f"wg{a}{m}", align_bytes=64) for m in range(M_TILES)] for a in range(PASSES)]
         w_codes = [keep.tile([P, M], U32, name=f"wc{a}", align_bytes=64) for a in range(PASSES)]
         w_scales = [keep.tile([P, M], U8, name=f"ws{a}", align_bytes=64) for a in range(PASSES)]
@@ -59,13 +59,16 @@ def tile_list_hboth_none_kernel(tc, xT, w, wgt, wgo, offs, offs2, out):
             nc.sync.dma_start(out=w_raw[a][:], in_=w_passes[a])
 
         def load_wgt(h):
-            nc.sync.dma_start(out=weights[h][:], in_=wgt[:, cols(h)])
+            nc.scalar.dma_start(out=weights[h][:], in_=wgt[:, cols(h)])
 
         def load_late():
             nc.sync.dma_start(out=late_weights[:], in_=wgt[:, cols(1)])
 
         gathered = [[keep.tile([P, PACK, N], F32, name=f"g{a}{h}") for h in range(HALVES)] for a in range(PASSES)]
-        grouped = [[keep.tile([P, N, PACK], BF16, name=f"gr{a}{h}", align_bytes=64) for h in range(HALVES)] for a in range(PASSES)]
+        grouped = [[keep.tile([P, N, PACK], BF16, name=f"gr{a}{h}", align_bytes=64) if a else None for h in range(HALVES)] for a in range(PASSES)]
+        grouped0 = keep.tile([P, S, PACK], BF16, name="gr0", align_bytes=64)
+        codes0 = keep.tile([P, S], U32, name="xc0", align_bytes=64)
+        scales0 = keep.tile([P, S], U8, name="xs0", align_bytes=64)
         halves = [keep.tile([P, N // 2, PACK], BF16, name=f"half{q}", align_bytes=64) for q in range(2)]
 
         def gather(a, i, h, late=None):
@@ -78,7 +81,7 @@ def tile_list_hboth_none_kernel(tc, xT, w, wgt, wgo, offs, offs2, out):
 
         def int_x(a, h, copy=nc.scalar.copy):
             copy(
-                out=grouped[a][h][:].rearrange("p (c j) i -> p c i j", j=4),
+                out=(grouped[a][h][:] if a else grouped0[:, cols(h), :]).rearrange("p (c j) i -> p c i j", j=4),
                 in_=gathered[a][h][:].rearrange("p i (c j) -> p c i j", j=4),
             )
 
@@ -102,6 +105,9 @@ def tile_list_hboth_none_kernel(tc, xT, w, wgt, wgo, offs, offs2, out):
         def quantize(codes, scales, src):
             nc.vector.quantize_mx(out=codes[:].bitcast(FP8X4), scales=scales[:], in_=src[:].rearrange("p n i -> p (n i)"))
 
+        def q_x0():
+            quantize(codes0, scales0, grouped0)
+
         def q_x(a, h):
             quantize(x_codes[a][h], x_scales[a][h], grouped[a][h])
 
@@ -115,8 +121,8 @@ def tile_list_hboth_none_kernel(tc, xT, w, wgt, wgo, offs, offs2, out):
                 out=accs[m][h][:],
                 lhsT=w_codes[a][:, m_cols].bitcast(FP8X4),
                 lhsT_scale=w_scales[a][:, m_cols],
-                rhs=x_codes[a][h][:].bitcast(FP8X4),
-                rhs_scale=x_scales[a][h][:],
+                rhs=(x_codes[a][h][:] if a else codes0[:, cols(h)]).bitcast(FP8X4),
+                rhs_scale=x_scales[a][h][:] if a else scales0[:, cols(h)],
                 start=(a == 0),
                 stop=(a == PASSES - 1),
             )
@@ -165,11 +171,10 @@ def tile_list_hboth_none_kernel(tc, xT, w, wgt, wgo, offs, offs2, out):
         int_x(0, 1)
         gather(1, 0, 0)
         gather(1, 0, 1)
-        q_x(0, 0)
         int_w(0)
         gather(1, 1, 0)
         gather(1, 1, 1)
-        q_x(0, 1)
+        q_x0()
         gather(1, 2, 0)
         gather(1, 2, 1)
         q_w(0)

from contextlib import ExitStack

import concourse.mybir as mybir

K, M, T, S = 1024, 256, 1024, 512
FLOPS = 2 * K * M * S

F32 = mybir.dt.float32
BF16 = mybir.dt.bfloat16
U32 = mybir.dt.uint32
U16 = mybir.dt.uint16
U8 = mybir.dt.uint8
FP8X4 = mybir.dt.float8_e4m3fn_x4
MULT = mybir.AluOpType.mult

P = 128
PACK = 4
PASSES = K // (P * PACK)
HALVES = 2
N = S // HALVES
M_TILES = M // P
LIST_COLS = N // 16


def tile_list_hboth_none_kernel(tc, xT, w, wgt, wgo, offs, offs2, out):
    nc = tc.nc
    x_planes = xT.rearrange("(a p i) t -> a i p t", a=PASSES, i=PACK)
    w_passes = w.rearrange("(a p i) n -> a p i n", a=PASSES, i=PACK)

    with ExitStack() as ctx:
        keep = ctx.enter_context(tc.tile_pool(name="keep", bufs=1))
        psum = ctx.enter_context(tc.psum_pool(name="psum", bufs=1))

        def cols(h):
            return slice(h * N, (h + 1) * N)

        offsets = keep.tile([P, S // 16], U16, name="offsets")
        offsets2 = keep.tile([P, S // 16], U16, name="offsets2")
        planes = [[keep.tile([P, T], F32, name=f"x{a}{i}") for i in range(PACK)] for a in range(PASSES)]
        weights = [keep.tile([P, N], F32, name=f"wgt{h}") for h in range(HALVES)]
        late_weights = keep.tile([P, N], F32, name="wgt1_late")
        w_raw = [keep.tile([P, PACK, M], F32, name=f"wraw{a}") for a in range(PASSES)]
        out_weights = keep.tile([P, S], F32, name="wgo_sb")
        placed = [keep.tile([P, T], F32, name=f"placed{m}") for m in range(M_TILES)]

        x_codes = [[keep.tile([P, N], U32, name=f"xc{a}{h}", align_bytes=64) if a else None for h in range(HALVES)] for a in range(PASSES)]
        x_scales = [[keep.tile([P, N], U8, name=f"xs{a}{h}", align_bytes=64) if a else None for h in range(HALVES)] for a in range(PASSES)]
        w_grouped = [[keep.tile([P, P, PACK], BF16, name=f"wg{a}{m}", align_bytes=64) for m in range(M_TILES)] for a in range(PASSES)]
        w_codes = [keep.tile([P, M], U32, name=f"wc{a}", align_bytes=64) for a in range(PASSES)]
        w_scales = [keep.tile([P, M], U8, name=f"ws{a}", align_bytes=64) for a in range(PASSES)]
        w_whole = keep.tile([P, M, PACK], BF16, name="w_whole", align_bytes=64)
        accs = [[psum.tile([P, N], F32, name=f"acc{m}{h}") for h in range(HALVES)] for m in range(M_TILES)]
        ys = [[keep.tile([P, N], F32, name=f"y{m}{h}") for h in range(HALVES)] for m in range(M_TILES)]

        def load_plane(a, i):
            nc.sync.dma_start(out=planes[a][i][:], in_=x_planes[a, i])

        def load_w(a):
            nc.sync.dma_start(out=w_raw[a][:], in_=w_passes[a])

        def load_wgt(h):
            nc.scalar.dma_start(out=weights[h][:], in_=wgt[:, cols(h)])

        def load_late():
            nc.sync.dma_start(out=late_weights[:], in_=wgt[:, cols(1)])

        gathered = [[keep.tile([P, PACK, N], F32, name=f"g{a}{h}") for h in range(HALVES)] for a in range(PASSES)]
        grouped = [[keep.tile([P, N, PACK], BF16, name=f"gr{a}{h}", align_bytes=64) if a else None for h in range(HALVES)] for a in range(PASSES)]
        grouped0 = keep.tile([P, S, PACK], BF16, name="gr0", align_bytes=64)
        codes0 = keep.tile([P, S], U32, name="xc0", align_bytes=64)
        scales0 = keep.tile([P, S], U8, name="xs0", align_bytes=64)
        halves = [keep.tile([P, N // 2, PACK], BF16, name=f"half{q}", align_bytes=64) for q in range(2)]

        def gather(a, i, h, late=None):
            nc.vector.tensor_tensor(
                gathered[a][h][:, i, :],
                planes[a][i][:].indirect(offsets[:, h * LIST_COLS : (h + 1) * LIST_COLS]),
                (weights[h] if late is None else late_weights)[:],
                MULT,
            )

        def int_x(a, h, copy=nc.scalar.copy):
            copy(
                out=(grouped[a][h][:] if a else grouped0[:, cols(h), :]).rearrange("p (c j) i -> p c i j", j=4),
                in_=gathered[a][h][:].rearrange("p i (c j) -> p c i j", j=4),
            )

        def int_half(q, copy):
            copy(
                out=halves[q][:].rearrange("p (c j) i -> p c i j", j=4),
                in_=gathered[1][0][:, :, q * 128 : (q + 1) * 128].rearrange("p i (c j) -> p c i j", j=4),
            )

        def q_half(q):
            c = slice(q * 128, (q + 1) * 128)
            quantize(x_codes[1][0][:, c], x_scales[1][0][:, c], halves[q])

        def int_w(a, m=None, copy=nc.scalar.copy):
            src = w_raw[a][:] if m is None else w_raw[a][:, :, m * P : (m + 1) * P]
            copy(
                out=(w_whole if m is None else w_grouped[a][m])[:].rearrange("p (c j) i -> p c i j", j=4),
                in_=src.rearrange("p i (c j) -> p c i j", j=4),
            )

        def quantize(codes, scales, src):
            nc.vector.quantize_mx(out=codes[:].bitcast(FP8X4), scales=scales[:], in_=src[:].rearrange("p n i -> p (n i)"))

        def q_x0():
            quantize(codes0, scales0, grouped0)

        def q_x(a, h):
            quantize(x_codes[a][h], x_scales[a][h], grouped[a][h])

        def q_w(a, m=None):
            c = slice(0, M) if m is None else slice(m * P, (m + 1) * P)
            quantize(w_codes[a][:, c], w_scales[a][:, c], w_whole if m is None else w_grouped[a][m])

        def mm(a, m, h):
            m_cols = slice(m * P, (m + 1) * P)
            nc.tensor.matmul_mx(
                out=accs[m][h][:],
                lhsT=w_codes[a][:, m_cols].bitcast(FP8X4),
                lhsT_scale=w_scales[a][:, m_cols],
                rhs=(x_codes[a][h][:] if a else codes0[:, cols(h)]).bitcast(FP8X4),
                rhs_scale=x_scales[a][h][:] if a else scales0[:, cols(h)],
                start=(a == 0),
                stop=(a == PASSES - 1),
            )

        def take(m, h, copy=nc.scalar.copy):
            copy(out=ys[m][h][:], in_=accs[m][h][:])

        def scatter(m, h):
            nc.vector.tensor_tensor(
                placed[m][:].indirect(offsets2[:, h * LIST_COLS : (h + 1) * LIST_COLS]),
                ys[m][h][:],
                out_weights[:, cols(h)],
                MULT,
            )

        def store(m):
            nc.sync.dma_start(out=out[m * P : (m + 1) * P, :], in_=placed[m][:])

        nc.sync.dma_start(offsets[:], offs)
        load_wgt(0)
        load_plane(0, 0)
        load_wgt(1)
        load_plane(0, 1)
        load_plane(0, 2)
        load_plane(0, 3)
        load_plane(1, 0)
        load_plane(1, 1)
        load_plane(1, 2)
        load_w(0)
        load_plane(1, 3)
        load_w(1)
        load_late()
        nc.sync.dma_start(offsets2[:], offs2)
        nc.sync.dma_start(out=out_weights[:], in_=wgo)
        nc.vector.memset(placed[0][:], 0.0)
        nc.vector.memset(placed[1][:], 0.0)
        gather(0, 0, 0)
        gather(0, 0, 1)
        gather(0, 1, 0)
        gather(0, 1, 1)
        gather(0, 2, 0)
        gather(0, 2, 1)
        gather(0, 3, 0)
        int_x(0, 0)
        gather(0, 3, 1)
        int_x(0, 1)
        gather(1, 0, 0)
        gather(1, 0, 1)
        int_w(0)
        gather(1, 1, 0)
        gather(1, 1, 1)
        q_x0()
        gather(1, 2, 0)
        gather(1, 2, 1)
        q_w(0)
        mm(0, 0, 0)
        mm(0, 1, 0)
        gather(1, 3, 0)
        int_half(0, nc.scalar.copy)
        int_half(1, nc.vector.tensor_copy)
        int_w(1, 0, nc.vector.tensor_copy)
        int_w(1, 1)
        q_w(1, 0)
        q_w(1, 1)
        q_half(1)
        q_half(0)
        mm(1, 0, 0)
        take(0, 0, nc.vector.tensor_copy)
        mm(1, 1, 0)
        take(1, 0)
        gather(1, 3, 1, "late")
        int_x(1, 1)
        mm(0, 0, 1)
        mm(0, 1, 1)
        scatter(0, 0)
        q_x(1, 1)
        mm(1, 0, 1)
        take(0, 1)
        mm(1, 1, 1)
        take(1, 1)
        scatter(1, 0)
        scatter(0, 1)
        store(0)
        scatter(1, 1)
        store(1)
